import numpy as np
import ml_dtypes


def mxq(x, axis, fmt="e4m3"):
    dtype, down = {"e4m3": (ml_dtypes.float8_e4m3fn, 7), "e5m2": (ml_dtypes.float8_e5m2, 14)}[fmt]
    v = np.moveaxis(np.asarray(x, np.float32).astype(ml_dtypes.bfloat16).astype(np.float64), axis, -1)
    blocks = v.reshape(v.shape[:-1] + (-1, 32))
    amax = np.abs(blocks).max(-1, keepdims=True)
    byte = np.maximum(np.where(amax > 0, np.frexp(amax)[1] - 1 + 127, 0) - down, 1)
    scale = np.exp2(byte - 127.0)
    codes = (blocks / scale).astype(np.float32).astype(dtype).astype(np.float64)
    return np.moveaxis((codes * scale).reshape(v.shape), -1, axis)


WIDE = False


def mx_kscale(k):
    if not WIDE:
        return np.ones(k)
    levels = np.array([10, -10, 5, -5, 0])
    if k % 512:
        return np.exp2(np.random.permutation(np.resize(levels, k // 32))).repeat(32)
    a = np.empty((k // 512, 16))
    for p in range(k // 512):
        a[p, :8] = np.random.permutation(np.resize(levels, 8))
        for g in range(8):
            far = levels[np.abs(levels - a[p, g]) >= 10]
            a[p, g + 8] = far[np.random.randint(len(far))]
    return np.exp2(a.ravel()).repeat(32)


def f64(x):
    return np.asarray(x).astype(np.float64)


def striped(idx):
    return np.tile(idx.reshape(-1, 16).T, (8, 1)).astype(np.uint16)


def unstriped(offs):
    return offs[:16].T.reshape(-1).astype(np.int64)


E2M1 = np.array([0.0, 0.5, 1.0, 1.5, 2.0, 3.0, 4.0, 6.0, -0.0, -0.5, -1.0, -1.5, -2.0, -3.0, -4.0, -6.0])


def pack_weight(w, fmt):
    k, n = w.shape
    w = f64(np.asarray(w, np.float32).astype(ml_dtypes.bfloat16)).reshape(k // 32, 32, n)
    amax = np.abs(w).max(1)
    if fmt == "e4m3":
        byte = np.frexp(amax)[1] - 1 + 127 - 7
    else:
        mant, ex = np.frexp(amax / 6.0)
        byte = np.where(mant > 0.5, ex, ex - 1) + 127
    byte = np.clip(np.where(amax > 0, byte, 1), 1, 254)
    scaled = (w * np.exp2(127.0 - byte)[:, None, :]).reshape(k, n).astype(np.float32)
    by_word = np.ascontiguousarray(scaled.reshape(k // 512, 128, 4, n).transpose(0, 1, 3, 2))
    if fmt == "e4m3":
        words = by_word.astype(ml_dtypes.float8_e4m3fn).view(np.uint8)
    else:
        c = by_word.astype(ml_dtypes.float4_e2m1fn).view(np.uint8) & 0xF
        words = (c[..., 0::2] | (c[..., 1::2] << 4)).reshape(k // 512, 128, 2 * n)
    return np.ascontiguousarray(words), np.ascontiguousarray(byte.astype(np.uint8).reshape(k // 512, 16, n))


def unpack_weight(words, scales, fmt):
    g, _, n = scales.shape
    words = np.ascontiguousarray(words).reshape(g, 128, n, -1)
    if fmt == "e4m3":
        vals = words.view(ml_dtypes.float8_e4m3fn).astype(np.float64)
    else:
        nib = np.empty((g, 128, n, 4), np.uint8)
        nib[..., 0::2] = words & 0xF
        nib[..., 1::2] = words >> 4
        vals = E2M1[nib]
    vals = vals * np.repeat(np.exp2(scales.astype(np.float64) - 127.0), 8, axis=1)[..., None]
    return vals.transpose(0, 1, 3, 2).reshape(g * 512, n)


def silu(v):
    return v / (1.0 + np.exp(-np.maximum(v, -700.0)))


K, T, E, C, H, N = 512, 768, 12, 128, 512, 128


def by_expert(wq, xq):
    return np.concatenate([wq[e].T @ xq[:, e * C:(e + 1) * C] for e in range(E)], axis=1)


def setup_inputs():
    n = np.random.standard_normal
    s = mx_kscale(K)
    u = mx_kscale(H)
    first = np.random.permutation(np.repeat(np.arange(E), T // E))
    second = (first + 1 + np.random.permutation(np.repeat(np.arange(E - 1), -(-T // (E - 1)))[:T])) % E
    while np.bincount(second, minlength=E).max() != T // E:
        load = np.bincount(second, minlength=E); hi, lo = int(load.argmax()), int(load.argmin())
        t = np.flatnonzero((second == hi) & (first != lo))[0]; second[t] = lo
    slot_token = np.empty(E * C, np.int64); pos = np.empty((2, T), np.int64); fill = np.zeros(E, np.int64)
    place = np.stack([np.random.permutation(C) for _ in range(E)])
    for r, deal in enumerate((first, second)):
        for t in np.random.permutation(T):
            e = deal[t]; j = e * C + place[e, fill[e]]; fill[e] += 1; slot_token[j] = t; pos[r, t] = j
    g = np.random.uniform(0.2, 0.8, T)
    partner = np.concatenate([np.random.permutation(T) for _ in range(-(-E * C // T))])[:E * C]
    x = pack_weight(n((K, T)) * s[:, None], "e4m3")
    w1 = [pack_weight(m, "e4m3") for m in n((E, K, H)) / np.sqrt(K) / s[None, :, None] * u]
    wp = [pack_weight(m, "e4m3") for m in n((E, K, H)) / np.sqrt(K) / s[None, :, None] * u]
    w2 = [pack_weight(m, "e4m3") for m in n((E, H, N)) / np.sqrt(H) / u[None, :, None]]
    return {
        "x_words": x[0],
        "x_scales": x[1],
        "w1_words": np.stack([m[0] for m in w1]),
        "w1_scales": np.stack([m[1] for m in w1]),
        "wp_words": np.stack([m[0] for m in wp]),
        "wp_scales": np.stack([m[1] for m in wp]),
        "w2_words": np.stack([m[0] for m in w2]),
        "w2_scales": np.stack([m[1] for m in w2]),
        "gate": np.stack([np.tile(g, (128, 1)), np.tile(1.0 - g, (128, 1))]).astype(np.float32),
        "offs": striped(slot_token),
        "pos1": striped(pos[0]),
        "pos2": striped(pos[1]),
        "offs2": striped(partner),
    }


def reference(x_words, x_scales, w1_words, w1_scales, wp_words, wp_scales, w2_words, w2_scales, gate, offs, pos1, pos2, offs2):
    w1 = np.stack([unpack_weight(w1_words[e], w1_scales[e], "e4m3") for e in range(E)])
    wp = np.stack([unpack_weight(wp_words[e], wp_scales[e], "e4m3") for e in range(E)])
    w2 = np.stack([unpack_weight(w2_words[e], w2_scales[e], "e4m3") for e in range(E)])
    idx, idx2 = unstriped(offs), unstriped(offs2)
    x = unpack_weight(x_words, x_scales, "e4m3")
    h = silu(by_expert(w1, x[:, idx]) + by_expert(wp, x[:, idx2]))
    y = by_expert(w2, mxq(h, 0, "e4m3"))
    out = sum(f64(gate[r, :1]) * y[:, unstriped(p)] for r, p in enumerate((pos1, pos2)))
    return out

@@ -1,0 +1,239 @@
+from contextlib import ExitStack
+
+import concourse.mybir as mybir
+from concourse.masks import make_identity
+
+K, T, E, C, H, N = 512, 768, 12, 128, 512, 128
+S = E * C
+P = 128
+FLOPS = 2 * S * (2 * K * H + H * N)
+
+F32 = mybir.dt.float32
+BF16 = mybir.dt.bfloat16
+I32 = mybir.dt.int32
+U32 = mybir.dt.uint32
+U16 = mybir.dt.uint16
+U8 = mybir.dt.uint8
+FP8X4 = mybir.dt.float8_e4m3fn_x4
+MULT = mybir.AluOpType.mult
+ADD = mybir.AluOpType.add
+SILU = mybir.ActivationFunctionType.Silu
+
+GATHER_RUNS = ((0, 2), (2, 5), (5, 8), (8, 10), (10, 12))
+TURN_RUNS = ((0, 2), (2, 4), (4, 6), (6, 8), (8, 10), (10, 11), (11, 12))
+QUANT_RUNS = ((0, 4), (4, 8), (8, 10), (10, 11), (11, 12))
+Y_RUNS = ((0, 4), (4, 8), (8, 11), (11, 12))
+OUT_RUNS = ((0, 512), (512, 768))
+
+
+def tile_moe_duo_silu_kernel(
+    tc, x_words, x_scales, w1_words, w1_scales, wp_words, wp_scales, w2_words, w2_scales, gate, offs, pos1, pos2, offs2, out
+):
+    nc = tc.nc
+    with ExitStack() as ctx:
+        keep = ctx.enter_context(tc.tile_pool(name="keep", bufs=1))
+        psum = ctx.enter_context(tc.psum_pool(name="psum", bufs=1))
+
+        offs_t = keep.tile([P, S // 16], U16, name="offs_t")
+        offs2_t = keep.tile([P, S // 16], U16, name="offs2_t")
+        pos1_t = keep.tile([P, T // 16], U16, name="pos1_t")
+        pos2_t = keep.tile([P, T // 16], U16, name="pos2_t")
+        xw = keep.tile([P, T], I32, name="xw", align_bytes=64)
+        xs = keep.tile([P, T], U8, name="xs", align_bytes=64)
+        wa = [keep.tile([P, E, H], I32, name=f"wa{a}", align_bytes=256) for a in range(2)]
+        ws = [[keep.tile([P, H], U8, name=f"ws{a}_{g}", align_bytes=256) for g in range(3)] for a in range(2)]
+        w2 = keep.tile([P, E, N], I32, name="w2", align_bytes=256)
+        w2s = keep.tile([P, E, N], U8, name="w2s", align_bytes=256)
+        gates = [keep.tile([P, T], F32, name=f"gate{r}") for r in range(2)]
+        ident = keep.tile([P, P], F32, name="ident", align_bytes=64)
+        warm = keep.tile([P, 2], F32, name="warm")
+        warm_out = keep.tile([P, 2], F32, name="warm_out")
+
+        words_in = (w1_words, wp_words)
+        scales_in = (w1_scales, wp_scales)
+
+        nc.vector.memset(xs[:].bitcast(I32), 0)
+        for g in range(3):
+            for a in range(2):
+                nc.vector.memset(ws[a][g][:].bitcast(I32), 0)
+        nc.vector.memset(w2s[:].rearrange("p e n -> p (e n)").bitcast(I32), 0)
+        nc.vector.memset(warm[:], 0.0)
+        nc.scalar.activation(warm_out[:], warm[:], SILU)
+
+        def load_words(a, e0, e1):
+            nc.sync.dma_start(
+                out=wa[a][:, e0:e1, :], in_=words_in[a][e0:e1, 0].rearrange("e p n t -> p e (n t)").bitcast(I32)
+            )
+
+        def load_scales(a, g, q):
+            nc.sync.dma_start(
+                out=ws[a][g][32 * q : 32 * q + 16, :].bitcast(I32),
+                in_=scales_in[a][4 * g : 4 * g + 4, 0, 4 * q : 4 * q + 4, :].bitcast(I32),
+            )
+
+        def load_xs(r):
+            nc.sync.dma_start(
+                out=xs[r:P:32, :].bitcast(I32), in_=x_scales[0].rearrange("(q r) t -> r q t", r=4)[r].bitcast(I32)
+            )
+
+        def load_w2s(r):
+            nc.gpsimd.dma_start(
+                out=w2s[r:P:32, :, :].bitcast(I32),
+                in_=w2_scales[:, 0].rearrange("e (q r) n -> r q e n", r=4)[r].bitcast(I32),
+            )
+
+        def load_w2(e0, e1):
+            nc.sync.dma_start(
+                out=w2[:, e0:e1, :], in_=w2_words[e0:e1, 0].rearrange("e p n t -> p e (n t)").bitcast(I32)
+            )
+
+        make_identity(nc, ident[:])
+        load_w2s(0)
+        load_w2s(1)
+        load_w2s(2)
+        load_w2s(3)
+        nc.sync.dma_start(offs_t[:], offs)
+        nc.sync.dma_start(out=xw[:], in_=x_words[0].rearrange("p t d -> p (t d)").bitcast(I32))
+        nc.sync.dma_start(offs2_t[:], offs2)
+        load_words(0, 0, 2)
+        load_xs(0)
+        load_xs(1)
+        load_xs(2)
+        load_xs(3)
+        load_words(1, 0, 2)
+        load_scales(0, 0, 0)
+        load_scales(0, 0, 1)
+        load_scales(0, 0, 2)
+        load_scales(0, 0, 3)
+        load_words(0, 2, 4)
+        load_scales(1, 0, 0)
+        load_scales(1, 0, 1)
+        load_scales(1, 0, 2)
+        load_scales(1, 0, 3)
+        load_words(1, 2, 4)
+        load_scales(0, 1, 0)
+        load_scales(0, 1, 1)
+        load_words(0, 4, 6)
+        load_scales(0, 1, 2)
+        load_scales(0, 1, 3)
+        load_words(1, 4, 6)
+        load_scales(1, 1, 0)
+        load_scales(1, 1, 1)
+        load_scales(1, 1, 2)
+        load_scales(1, 1, 3)
+        load_words(0, 6, 8)
+        load_scales(0, 2, 0)
+        load_scales(0, 2, 1)
+        load_words(1, 6, 8)
+        load_scales(0, 2, 2)
+        load_scales(0, 2, 3)
+        load_words(0, 8, 10)
+        load_scales(1, 2, 0)
+        load_scales(1, 2, 1)
+        load_scales(1, 2, 2)
+        load_scales(1, 2, 3)
+        load_words(1, 8, 10)
+        load_words(0, 10, 12)
+        load_words(1, 10, 11)
+        load_words(1, 11, 12)
+        load_w2(0, 4)
+        nc.sync.dma_start(pos1_t[:], pos1)
+        load_w2(4, 8)
+        nc.sync.dma_start(pos2_t[:], pos2)
+        load_w2(8, 12)
+        nc.sync.dma_start(out=gates[0][:], in_=gate[0])
+        nc.sync.dma_start(out=gates[1][:], in_=gate[1])
+
+        lists = (offs_t, offs2_t)
+        gw = {}
+        gs = {}
+        for e0, e1 in GATHER_RUNS:
+            width = (e1 - e0) * C
+            cols = slice(e0 * C // 16, e1 * C // 16)
+            made = []
+            for a in range(2):
+                words = keep.tile([P, width], U32, name=f"gw{a}_{e0}", align_bytes=256)
+                nc.vector.tensor_copy(words[:], xw[:].bitcast(U32).indirect(lists[a][:, cols]))
+                made.append(words)
+            for a in range(2):
+                scales = keep.tile([P, width], U8, name=f"gs{a}_{e0}", align_bytes=256)
+                nc.vector.tensor_copy(scales[:], xs[:].indirect(lists[a][:, cols]))
+                for e in range(e0, e1):
+                    mine = slice((e - e0) * C, (e - e0 + 1) * C)
+                    gw[a, e] = made[a][:, mine]
+                    gs[a, e] = scales[:, mine]
+
+        hq = {}
+        for e0, e1 in QUANT_RUNS:
+            tile = keep.tile([P, (e1 - e0) * C * 4], BF16, name=f"hq{e0}", align_bytes=256)
+            for e in range(e0, e1):
+                hq[e] = (tile, e - e0)
+        for e0, e1 in TURN_RUNS:
+            hs = []
+            for e in range(e0, e1):
+                acc = psum.tile([P, H], F32, name="acc", tag="acc", bufs=3)
+                g, j = divmod(e, 4)
+                for a in range(2):
+                    nc.tensor.matmul_mx(
+                        out=acc[:],
+                        lhsT=gw[a, e].bitcast(FP8X4),
+                        lhsT_scale=gs[a, e],
+                        rhs=wa[a][:, e, :].bitcast(FP8X4),
+                        rhs_scale=ws[a][g][4 * j :, :],
+                        start=(a == 0),
+                        stop=(a == 1),
+                    )
+                h = keep.tile([P, H], BF16, name=f"h{e}", align_bytes=256)
+                nc.scalar.activation(
+                    h[:].rearrange("s (u p d) -> s u p d", u=2, d=2), acc[:].rearrange("s (p u d) -> s u p d", u=2, d=2), SILU
+                )
+                hs.append(h)
+            turned = psum.tile([P, 2, 2, C], F32, name="turned", tag="turned", bufs=2)
+            for x, h in enumerate(hs):
+                for u in range(2):
+                    nc.tensor.transpose(turned[:, x, u, :], h[:].bitcast(F32)[:, u * P : (u + 1) * P], ident[:])
+            tile, first = hq[e0]
+            count = e1 - e0
+            nc.scalar.copy(
+                tile[:].bitcast(F32)[:, first * 2 * C : (first + count) * 2 * C].rearrange("p (x s u) -> p x s u", x=count, u=2),
+                turned[:, 0:count].rearrange("p x u s -> p x s u"),
+            )
+
+        y = keep.tile([P, S], F32, name="y")
+        hc = {}
+        for e0, e1 in QUANT_RUNS:
+            width = (e1 - e0) * C
+            codes = keep.tile([P, width], U32, name=f"hc{e0}", align_bytes=256)
+            scales = keep.tile([P, width], U8, name=f"hsc{e0}", align_bytes=256)
+            nc.vector.quantize_mx(out=codes[:].bitcast(FP8X4), scales=scales[:], in_=hq[e0][0][:])
+            for e in range(e0, e1):
+                mine = slice((e - e0) * C, (e - e0 + 1) * C)
+                hc[e] = (codes[:, mine], scales[:, mine])
+        for e0, e1 in Y_RUNS:
+            bank = psum.tile([P, 4 * C], F32, name="bank", tag="bank", bufs=3)
+            for e in range(e0, e1):
+                nc.tensor.matmul_mx(
+                    out=bank[:, (e - e0) * C : (e - e0 + 1) * C],
+                    lhsT=w2[:, e, :].bitcast(FP8X4),
+                    lhsT_scale=w2s[:, e, :],
+                    rhs=hc[e][0].bitcast(FP8X4),
+                    rhs_scale=hc[e][1],
+                    start=True,
+                    stop=True,
+                )
+            if e0 == 8:
+                nc.scalar.copy(y[:, e0 * C : e1 * C], bank[:, 0 : (e1 - e0) * C])
+            else:
+                nc.vector.tensor_copy(y[:, e0 * C : e1 * C], bank[:, 0 : (e1 - e0) * C])
+
+        first = keep.tile([P, T], F32, name="first")
+        nc.vector.tensor_tensor(first[:], y[:].indirect(pos1_t[:]), gates[0][:], MULT)
+        seconds = []
+        for t0, t1 in OUT_RUNS:
+            second = keep.tile([P, t1 - t0], F32, name=f"second{t0}")
+            nc.vector.tensor_tensor(second[:], y[:].indirect(pos2_t[:, t0 // 16 : t1 // 16]), gates[1][:, t0:t1], MULT)
+            seconds.append(second)
+        for (t0, t1), second in zip(OUT_RUNS, seconds):
+            total = keep.tile([P, t1 - t0], F32, name=f"total{t0}")
+            nc.vector.tensor_tensor(total[:], first[:, t0:t1], second[:], ADD)
+            nc.sync.dma_start(out=out[:, t0:t1], in_=total[:])

@@ -19,9 +19,9 @@ MULT = mybir.AluOpType.mult
 ADD = mybir.AluOpType.add
 SILU = mybir.ActivationFunctionType.Silu
 
-GATHER_RUNS = ((0, 2), (2, 5), (5, 8), (8, 10), (10, 12))
-TURN_RUNS = ((0, 2), (2, 4), (4, 6), (6, 8), (8, 10), (10, 11), (11, 12))
-QUANT_RUNS = ((0, 4), (4, 8), (8, 10), (10, 11), (11, 12))
+GATHER_RUNS = ((0, 4), (4, 6), (6, 8), (8, 10), (10, 11), (11, 12))
+TURN_RUNS = ((0, 1), (1, 3), (3, 5), (5, 7), (7, 9), (9, 11), (11, 12))
+QUANT_RUNS = ((0, 1), (1, 5), (5, 9), (9, 11), (11, 12))
 Y_RUNS = ((0, 4), (4, 8), (8, 11), (11, 12))
 OUT_RUNS = ((0, 512), (512, 768))
 
@@ -46,19 +46,15 @@ def tile_moe_duo_silu_kernel(
         w2s = keep.tile([P, E, N], U8, name="w2s", align_bytes=256)
         gates = [keep.tile([P, T], F32, name=f"gate{r}") for r in range(2)]
         ident = keep.tile([P, P], F32, name="ident", align_bytes=64)
-        warm = keep.tile([P, 2], F32, name="warm")
-        warm_out = keep.tile([P, 2], F32, name="warm_out")
 
         words_in = (w1_words, wp_words)
         scales_in = (w1_scales, wp_scales)
 
-        nc.vector.memset(xs[:].bitcast(I32), 0)
+        nc.gpsimd.memset(xs[:].bitcast(I32), 0)
         for g in range(3):
             for a in range(2):
-                nc.vector.memset(ws[a][g][:].bitcast(I32), 0)
-        nc.vector.memset(w2s[:].rearrange("p e n -> p (e n)").bitcast(I32), 0)
-        nc.vector.memset(warm[:], 0.0)
-        nc.scalar.activation(warm_out[:], warm[:], SILU)
+                nc.gpsimd.memset(ws[a][g][:].bitcast(I32), 0)
+        nc.gpsimd.memset(w2s[:].rearrange("p e n -> p (e n)").bitcast(I32), 0)
 
         def load_words(a, e0, e1):
             nc.sync.dma_start(
@@ -66,13 +62,15 @@ def tile_moe_duo_silu_kernel(
             )
 
         def load_scales(a, g, q):
-            nc.sync.dma_start(
+            queue = nc.sync
+            queue.dma_start(
                 out=ws[a][g][32 * q : 32 * q + 16, :].bitcast(I32),
                 in_=scales_in[a][4 * g : 4 * g + 4, 0, 4 * q : 4 * q + 4, :].bitcast(I32),
             )
 
         def load_xs(r):
-            nc.sync.dma_start(
+            queue = nc.sync if r < 2 else nc.scalar
+            queue.dma_start(
                 out=xs[r:P:32, :].bitcast(I32), in_=x_scales[0].rearrange("(q r) t -> r q t", r=4)[r].bitcast(I32)
             )
 
@@ -87,55 +85,54 @@ def tile_moe_duo_silu_kernel(
                 out=w2[:, e0:e1, :], in_=w2_words[e0:e1, 0].rearrange("e p n t -> p e (n t)").bitcast(I32)
             )
 
+        load_xs(2)
+        load_xs(3)
         make_identity(nc, ident[:])
         load_w2s(0)
         load_w2s(1)
         load_w2s(2)
         load_w2s(3)
-        nc.sync.dma_start(offs_t[:], offs)
         nc.sync.dma_start(out=xw[:], in_=x_words[0].rearrange("p t d -> p (t d)").bitcast(I32))
-        nc.sync.dma_start(offs2_t[:], offs2)
-        load_words(0, 0, 2)
         load_xs(0)
         load_xs(1)
-        load_xs(2)
-        load_xs(3)
-        load_words(1, 0, 2)
-        load_scales(0, 0, 0)
-        load_scales(0, 0, 1)
-        load_scales(0, 0, 2)
-        load_scales(0, 0, 3)
-        load_words(0, 2, 4)
+        nc.sync.dma_start(offs_t[:], offs)
+        nc.sync.dma_start(offs2_t[:], offs2)
+        load_words(1, 0, 4)
         load_scales(1, 0, 0)
         load_scales(1, 0, 1)
         load_scales(1, 0, 2)
         load_scales(1, 0, 3)
-        load_words(1, 2, 4)
-        load_scales(0, 1, 0)
-        load_scales(0, 1, 1)
-        load_words(0, 4, 6)
-        load_scales(0, 1, 2)
-        load_scales(0, 1, 3)
-        load_words(1, 4, 6)
+        load_scales(0, 0, 0)
+        load_scales(0, 0, 1)
+        load_words(0, 0, 4)
+        load_scales(0, 0, 2)
+        load_scales(0, 0, 3)
         load_scales(1, 1, 0)
         load_scales(1, 1, 1)
         load_scales(1, 1, 2)
         load_scales(1, 1, 3)
+        load_words(1, 4, 8)
+        load_scales(0, 1, 0)
+        load_scales(0, 1, 1)
+        load_scales(0, 1, 2)
+        load_scales(0, 1, 3)
+        load_words(0, 4, 6)
         load_words(0, 6, 8)
-        load_scales(0, 2, 0)
-        load_scales(0, 2, 1)
-        load_words(1, 6, 8)
-        load_scales(0, 2, 2)
-        load_scales(0, 2, 3)
-        load_words(0, 8, 10)
         load_scales(1, 2, 0)
         load_scales(1, 2, 1)
         load_scales(1, 2, 2)
         load_scales(1, 2, 3)
         load_words(1, 8, 10)
-        load_words(0, 10, 12)
+        load_words(0, 8, 9)
+        load_scales(0, 2, 0)
+        load_scales(0, 2, 1)
+        load_scales(0, 2, 2)
+        load_scales(0, 2, 3)
+        load_words(0, 9, 10)
         load_words(1, 10, 11)
+        load_words(0, 10, 11)
         load_words(1, 11, 12)
+        load_words(0, 11, 12)
         load_w2(0, 4)
         nc.sync.dma_start(pos1_t[:], pos1)
         load_w2(4, 8)
@@ -150,17 +147,14 @@ def tile_moe_duo_silu_kernel(
         for e0, e1 in GATHER_RUNS:
             width = (e1 - e0) * C
             cols = slice(e0 * C // 16, e1 * C // 16)
-            made = []
             for a in range(2):
                 words = keep.tile([P, width], U32, name=f"gw{a}_{e0}", align_bytes=256)
                 nc.vector.tensor_copy(words[:], xw[:].bitcast(U32).indirect(lists[a][:, cols]))
-                made.append(words)
-            for a in range(2):
                 scales = keep.tile([P, width], U8, name=f"gs{a}_{e0}", align_bytes=256)
                 nc.vector.tensor_copy(scales[:], xs[:].indirect(lists[a][:, cols]))
                 for e in range(e0, e1):
                     mine = slice((e - e0) * C, (e - e0 + 1) * C)
-                    gw[a, e] = made[a][:, mine]
+                    gw[a, e] = words[:, mine]
                     gs[a, e] = scales[:, mine]
 
         hq = {}
@@ -194,7 +188,8 @@ def tile_moe_duo_silu_kernel(
                     nc.tensor.transpose(turned[:, x, u, :], h[:].bitcast(F32)[:, u * P : (u + 1) * P], ident[:])
             tile, first = hq[e0]
             count = e1 - e0
-            nc.scalar.copy(
+            move = nc.vector.tensor_copy if e0 in (9,) else nc.scalar.copy
+            move(
                 tile[:].bitcast(F32)[:, first * 2 * C : (first + count) * 2 * C].rearrange("p (x s u) -> p x s u", x=count, u=2),
                 turned[:, 0:count].rearrange("p x u s -> p x s u"),
             )
@@ -221,7 +216,7 @@ def tile_moe_duo_silu_kernel(
                     start=True,
                     stop=True,
                 )
-            if e0 == 8:
+            if e1 < E:
                 nc.scalar.copy(y[:, e0 * C : e1 * C], bank[:, 0 : (e1 - e0) * C])
             else:
                 nc.vector.tensor_copy(y[:, e0 * C : e1 * C], bank[:, 0 : (e1 - e0) * C])

@@ -19,11 +19,16 @@ MULT = mybir.AluOpType.mult
 ADD = mybir.AluOpType.add
 SILU = mybir.ActivationFunctionType.Silu
 
-GATHER_RUNS = ((0, 4), (4, 6), (6, 8), (8, 10), (10, 11), (11, 12))
-TURN_RUNS = ((0, 1), (1, 3), (3, 5), (5, 7), (7, 9), (9, 11), (11, 12))
-QUANT_RUNS = ((0, 1), (1, 5), (5, 9), (9, 11), (11, 12))
-Y_RUNS = ((0, 4), (4, 8), (8, 11), (11, 12))
-OUT_RUNS = ((0, 512), (512, 768))
+GATHERS = (("w", 0, 0, 3), ("s", 0, 0, 3), ("w", 1, 0, 3), ("s", 1, 0, 3), ("w", 0, 3, 6), ("s", 0, 3, 6), ("w", 1, 3, 6), ("s", 1, 3, 6), ("w", 0, 6, 9), ("s", 0, 6, 9), ("w", 1, 6, 9), ("s", 1, 6, 9), ("s", 0, 9, 12), ("s", 1, 9, 12), ("w", 0, 9, 10), ("w", 1, 9, 10), ("w", 0, 10, 11), ("w", 1, 10, 11), ("w", 0, 11, 12), ("w", 1, 11, 12))
+TRIPLES = ((0, 3), (3, 6), (6, 9), (9, 12))
+TURNS_AFTER = (((0, 1, 6),), ((1, 3, 3), (3, 4, 6)), ((4, 6, 0), (6, 7, 6)), ((7, 9, 3), (9, 11, 6), (11, 12, 4)))
+VECTOR_TURNS = (7,)
+Y_BANKS = (1, 2, 0, 7)
+VECTOR_Y = (11,)
+BANK = 2048
+QUANT_RUNS = ((0, 4), (4, 6), (6, 7), (7, 9), (9, 11), (11, 12))
+Y_RUNS = ((0, 4), (4, 7), (7, 11), (11, 12))
+OUT_RUNS = ((0, 384), (384, 640), (640, 768))
 
 
 def tile_moe_duo_silu_kernel(
@@ -103,35 +108,34 @@ def tile_moe_duo_silu_kernel(
         load_scales(1, 0, 2)
         load_scales(1, 0, 3)
         load_scales(0, 0, 0)
+        load_words(0, 0, 3)
         load_scales(0, 0, 1)
-        load_words(0, 0, 4)
         load_scales(0, 0, 2)
         load_scales(0, 0, 3)
         load_scales(1, 1, 0)
         load_scales(1, 1, 1)
+        load_words(1, 4, 7)
         load_scales(1, 1, 2)
         load_scales(1, 1, 3)
-        load_words(1, 4, 8)
         load_scales(0, 1, 0)
         load_scales(0, 1, 1)
         load_scales(0, 1, 2)
         load_scales(0, 1, 3)
-        load_words(0, 4, 6)
-        load_words(0, 6, 8)
+        load_words(0, 3, 6)
         load_scales(1, 2, 0)
         load_scales(1, 2, 1)
         load_scales(1, 2, 2)
         load_scales(1, 2, 3)
-        load_words(1, 8, 10)
-        load_words(0, 8, 9)
+        load_words(1, 7, 10)
         load_scales(0, 2, 0)
         load_scales(0, 2, 1)
         load_scales(0, 2, 2)
         load_scales(0, 2, 3)
+        load_words(0, 6, 8)
+        load_words(0, 8, 9)
+        load_words(1, 10, 12)
         load_words(0, 9, 10)
-        load_words(1, 10, 11)
         load_words(0, 10, 11)
-        load_words(1, 11, 12)
         load_words(0, 11, 12)
         load_w2(0, 4)
         nc.sync.dma_start(pos1_t[:], pos1)
@@ -144,28 +148,22 @@ def tile_moe_duo_silu_kernel(
         lists = (offs_t, offs2_t)
         gw = {}
         gs = {}
-        for e0, e1 in GATHER_RUNS:
-            width = (e1 - e0) * C
-            cols = slice(e0 * C // 16, e1 * C // 16)
-            for a in range(2):
-                words = keep.tile([P, width], U32, name=f"gw{a}_{e0}", align_bytes=256)
-                nc.vector.tensor_copy(words[:], xw[:].bitcast(U32).indirect(lists[a][:, cols]))
-                scales = keep.tile([P, width], U8, name=f"gs{a}_{e0}", align_bytes=256)
-                nc.vector.tensor_copy(scales[:], xs[:].indirect(lists[a][:, cols]))
-                for e in range(e0, e1):
-                    mine = slice((e - e0) * C, (e - e0 + 1) * C)
-                    gw[a, e] = words[:, mine]
-                    gs[a, e] = scales[:, mine]
+        for kind, a, e0, e1 in GATHERS:
+            offsets = lists[a][:, e0 * C // 16 : e1 * C // 16]
+            if kind == "w":
+                got = keep.tile([P, (e1 - e0) * C], U32, name=f"gw{a}_{e0}", align_bytes=256)
+                nc.vector.tensor_copy(got[:], xw[:].bitcast(U32).indirect(offsets))
+            else:
+                got = keep.tile([P, (e1 - e0) * C], U8, name=f"gs{a}_{e0}", align_bytes=256)
+                nc.vector.tensor_copy(got[:], xs[:].indirect(offsets))
+            for e in range(e0, e1):
+                (gw if kind == "w" else gs)[a, e] = got[:, (e - e0) * C : (e - e0 + 1) * C]
 
-        hq = {}
-        for e0, e1 in QUANT_RUNS:
-            tile = keep.tile([P, (e1 - e0) * C * 4], BF16, name=f"hq{e0}", align_bytes=256)
-            for e in range(e0, e1):
-                hq[e] = (tile, e - e0)
-        for e0, e1 in TURN_RUNS:
-            hs = []
-            for e in range(e0, e1):
-                acc = psum.tile([P, H], F32, name="acc", tag="acc", bufs=3)
+        hq = keep.tile([P, S * 4], BF16, name="hq", align_bytes=256)
+        hs = {}
+        for (first_e, last_e), turns in zip(TRIPLES, TURNS_AFTER):
+            for e in range(first_e, last_e):
+                acc = psum.tile([P, H], F32, name=f"acc{e}", offset=(e % 6) * BANK)
                 g, j = divmod(e, 4)
                 for a in range(2):
                     nc.tensor.matmul_mx(
@@ -181,18 +179,18 @@ def tile_moe_duo_silu_kernel(
                 nc.scalar.activation(
                     h[:].rearrange("s (u p d) -> s u p d", u=2, d=2), acc[:].rearrange("s (p u d) -> s u p d", u=2, d=2), SILU
                 )
-                hs.append(h)
-            turned = psum.tile([P, 2, 2, C], F32, name="turned", tag="turned", bufs=2)
-            for x, h in enumerate(hs):
-                for u in range(2):
-                    nc.tensor.transpose(turned[:, x, u, :], h[:].bitcast(F32)[:, u * P : (u + 1) * P], ident[:])
-            tile, first = hq[e0]
-            count = e1 - e0
-            move = nc.vector.tensor_copy if e0 in (9,) else nc.scalar.copy
-            move(
-                tile[:].bitcast(F32)[:, first * 2 * C : (first + count) * 2 * C].rearrange("p (x s u) -> p x s u", x=count, u=2),
-                turned[:, 0:count].rearrange("p x u s -> p x s u"),
-            )
+                hs[e] = h
+            for e0, e1, bank_no in turns:
+                count = e1 - e0
+                turned = psum.tile([P, count, 2, C], F32, name=f"turned{e0}", offset=bank_no * BANK)
+                for e in range(e0, e1):
+                    for u in range(2):
+                        nc.tensor.transpose(turned[:, e - e0, u, :], hs[e][:].bitcast(F32)[:, u * P : (u + 1) * P], ident[:])
+                move = nc.vector.tensor_copy if e0 in VECTOR_TURNS else nc.scalar.copy
+                move(
+                    hq[:].bitcast(F32)[:, e0 * 2 * C : e1 * 2 * C].rearrange("p (x s u) -> p x s u", x=count, u=2),
+                    turned[:].rearrange("p x u s -> p x s u"),
+                )
 
         y = keep.tile([P, S], F32, name="y")
         hc = {}
@@ -200,12 +198,12 @@ def tile_moe_duo_silu_kernel(
             width = (e1 - e0) * C
             codes = keep.tile([P, width], U32, name=f"hc{e0}", align_bytes=256)
             scales = keep.tile([P, width], U8, name=f"hsc{e0}", align_bytes=256)
-            nc.vector.quantize_mx(out=codes[:].bitcast(FP8X4), scales=scales[:], in_=hq[e0][0][:])
+            nc.vector.quantize_mx(out=codes[:].bitcast(FP8X4), scales=scales[:], in_=hq[:, e0 * 4 * C : e1 * 4 * C])
             for e in range(e0, e1):
                 mine = slice((e - e0) * C, (e - e0 + 1) * C)
                 hc[e] = (codes[:, mine], scales[:, mine])
-        for e0, e1 in Y_RUNS:
-            bank = psum.tile([P, 4 * C], F32, name="bank", tag="bank", bufs=3)
+        for (e0, e1), bank_no in zip(Y_RUNS, Y_BANKS):
+            bank = psum.tile([P, (e1 - e0) * C], F32, name=f"ybank{e0}", offset=bank_no * BANK)
             for e in range(e0, e1):
                 nc.tensor.matmul_mx(
                     out=bank[:, (e - e0) * C : (e - e0 + 1) * C],
@@ -216,19 +214,25 @@ def tile_moe_duo_silu_kernel(
                     start=True,
                     stop=True,
                 )
-            if e1 < E:
-                nc.scalar.copy(y[:, e0 * C : e1 * C], bank[:, 0 : (e1 - e0) * C])
-            else:
-                nc.vector.tensor_copy(y[:, e0 * C : e1 * C], bank[:, 0 : (e1 - e0) * C])
+            move = nc.vector.tensor_copy if e0 in VECTOR_Y else nc.scalar.copy
+            move(y[:, e0 * C : e1 * C], bank[:])
 
         first = keep.tile([P, T], F32, name="first")
         nc.vector.tensor_tensor(first[:], y[:].indirect(pos1_t[:]), gates[0][:], MULT)
-        seconds = []
-        for t0, t1 in OUT_RUNS:
+        seconds = {}
+
+        def gather_second(t0, t1):
             second = keep.tile([P, t1 - t0], F32, name=f"second{t0}")
             nc.vector.tensor_tensor(second[:], y[:].indirect(pos2_t[:, t0 // 16 : t1 // 16]), gates[1][:, t0:t1], MULT)
-            seconds.append(second)
-        for (t0, t1), second in zip(OUT_RUNS, seconds):
+            seconds[t0] = second
+
+        def add_and_store(t0, t1):
             total = keep.tile([P, t1 - t0], F32, name=f"total{t0}")
-            nc.vector.tensor_tensor(total[:], first[:, t0:t1], second[:], ADD)
+            nc.vector.tensor_tensor(total[:], first[:, t0:t1], seconds[t0][:], ADD)
             nc.sync.dma_start(out=out[:, t0:t1], in_=total[:])
+
+        gather_second(*OUT_RUNS[0])
+        for done, ahead in zip(OUT_RUNS, OUT_RUNS[1:]):
+            gather_second(*ahead)
+            add_and_store(*done)
+        add_and_store(*OUT_RUNS[-1])

@@ -19,15 +19,17 @@ MULT = mybir.AluOpType.mult
 ADD = mybir.AluOpType.add
 SILU = mybir.ActivationFunctionType.Silu
 
-GATHERS = (("w", 0, 0, 3), ("s", 0, 0, 3), ("w", 1, 0, 3), ("s", 1, 0, 3), ("w", 0, 3, 6), ("s", 0, 3, 6), ("w", 1, 3, 6), ("s", 1, 3, 6), ("w", 0, 6, 9), ("s", 0, 6, 9), ("w", 1, 6, 9), ("s", 1, 6, 9), ("s", 0, 9, 12), ("s", 1, 9, 12), ("w", 0, 9, 10), ("w", 1, 9, 10), ("w", 0, 10, 11), ("w", 1, 10, 11), ("w", 0, 11, 12), ("w", 1, 11, 12))
-TRIPLES = ((0, 3), (3, 6), (6, 9), (9, 12))
-TURNS_AFTER = (((0, 1, 6),), ((1, 3, 3), (3, 4, 6)), ((4, 6, 0), (6, 7, 6)), ((7, 9, 3), (9, 11, 6), (11, 12, 4)))
-VECTOR_TURNS = (7,)
-Y_BANKS = (1, 2, 0, 7)
-VECTOR_Y = (11,)
+TOKEN, PARTNER = 0, 1
 BANK = 2048
-QUANT_RUNS = ((0, 4), (4, 6), (6, 7), (7, 9), (9, 11), (11, 12))
-Y_RUNS = ((0, 4), (4, 7), (7, 11), (11, 12))
+PLANE = {TOKEN: 0, PARTNER: 4}
+W2_PLANE = 8
+QUANT_RUNS = ((0, 4), (4, 8), (8, 10), (10, 11), (11, 12))
+Y_RUNS = ((0, 4), (4, 8), (8, 11), (11, 12))
+SCALAR_Y = (4, 8)
+Y_BANKS = (0, 1, 2, 3)
+HALF = H // 2
+QUAD = 4
+VECTOR_TURNS = (8, 9)
 OUT_RUNS = ((0, 384), (384, 640), (640, 768))
 
 
@@ -46,19 +48,17 @@ def tile_moe_duo_silu_kernel(
         xw = keep.tile([P, T], I32, name="xw", align_bytes=64)
         xs = keep.tile([P, T], U8, name="xs", align_bytes=64)
         wa = [keep.tile([P, E, H], I32, name=f"wa{a}", align_bytes=256) for a in range(2)]
-        ws = [[keep.tile([P, H], U8, name=f"ws{a}_{g}", align_bytes=256) for g in range(3)] for a in range(2)]
+        ws = [keep.tile([P, E, H], U8, name=f"ws{a}", align_bytes=256) for a in range(2)]
         w2 = keep.tile([P, E, N], I32, name="w2", align_bytes=256)
         w2s = keep.tile([P, E, N], U8, name="w2s", align_bytes=256)
         gates = [keep.tile([P, T], F32, name=f"gate{r}") for r in range(2)]
         ident = keep.tile([P, P], F32, name="ident", align_bytes=64)
 
         words_in = (w1_words, wp_words)
-        scales_in = (w1_scales, wp_scales)
 
         nc.gpsimd.memset(xs[:].bitcast(I32), 0)
-        for g in range(3):
-            for a in range(2):
-                nc.gpsimd.memset(ws[a][g][:].bitcast(I32), 0)
+        nc.vector.memset(ws[PARTNER][:].rearrange("p e n -> p (e n)").bitcast(I32), 0)
+        nc.gpsimd.memset(ws[TOKEN][:].rearrange("p e n -> p (e n)").bitcast(I32), 0)
         nc.gpsimd.memset(w2s[:].rearrange("p e n -> p (e n)").bitcast(I32), 0)
 
         def load_words(a, e0, e1):
@@ -66,23 +66,17 @@ def tile_moe_duo_silu_kernel(
                 out=wa[a][:, e0:e1, :], in_=words_in[a][e0:e1, 0].rearrange("e p n t -> p e (n t)").bitcast(I32)
             )
 
-        def load_scales(a, g, q):
-            queue = nc.sync
-            queue.dma_start(
-                out=ws[a][g][32 * q : 32 * q + 16, :].bitcast(I32),
-                in_=scales_in[a][4 * g : 4 * g + 4, 0, 4 * q : 4 * q + 4, :].bitcast(I32),
-            )
+        def load_scale_rows(queue, plane, first, source):
+            for r in range(4):
+                queue.dma_start(
+                    out=plane[first + r : P : 32, :, :].bitcast(I32),
+                    in_=source[:, 0].rearrange("e (q r) n -> r q e n", r=4)[r].bitcast(I32),
+                )
 
         def load_xs(r):
             queue = nc.sync if r < 2 else nc.scalar
             queue.dma_start(
                 out=xs[r:P:32, :].bitcast(I32), in_=x_scales[0].rearrange("(q r) t -> r q t", r=4)[r].bitcast(I32)
-            )
-
-        def load_w2s(r):
-            nc.gpsimd.dma_start(
-                out=w2s[r:P:32, :, :].bitcast(I32),
-                in_=w2_scales[:, 0].rearrange("e (q r) n -> r q e n", r=4)[r].bitcast(I32),
             )
 
         def load_w2(e0, e1):
@@ -93,50 +87,23 @@ def tile_moe_duo_silu_kernel(
         load_xs(2)
         load_xs(3)
         make_identity(nc, ident[:])
-        load_w2s(0)
-        load_w2s(1)
-        load_w2s(2)
-        load_w2s(3)
+        load_scale_rows(nc.gpsimd, w2s, W2_PLANE, w2_scales)
         nc.sync.dma_start(out=xw[:], in_=x_words[0].rearrange("p t d -> p (t d)").bitcast(I32))
         load_xs(0)
         load_xs(1)
-        nc.sync.dma_start(offs_t[:], offs)
         nc.sync.dma_start(offs2_t[:], offs2)
-        load_words(1, 0, 4)
-        load_scales(1, 0, 0)
-        load_scales(1, 0, 1)
-        load_scales(1, 0, 2)
-        load_scales(1, 0, 3)
-        load_scales(0, 0, 0)
-        load_words(0, 0, 3)
-        load_scales(0, 0, 1)
-        load_scales(0, 0, 2)
-        load_scales(0, 0, 3)
-        load_scales(1, 1, 0)
-        load_scales(1, 1, 1)
-        load_words(1, 4, 7)
-        load_scales(1, 1, 2)
-        load_scales(1, 1, 3)
-        load_scales(0, 1, 0)
-        load_scales(0, 1, 1)
-        load_scales(0, 1, 2)
-        load_scales(0, 1, 3)
-        load_words(0, 3, 6)
-        load_scales(1, 2, 0)
-        load_scales(1, 2, 1)
-        load_scales(1, 2, 2)
-        load_scales(1, 2, 3)
-        load_words(1, 7, 10)
-        load_scales(0, 2, 0)
-        load_scales(0, 2, 1)
-        load_scales(0, 2, 2)
-        load_scales(0, 2, 3)
-        load_words(0, 6, 8)
-        load_words(0, 8, 9)
-        load_words(1, 10, 12)
-        load_words(0, 9, 10)
-        load_words(0, 10, 11)
-        load_words(0, 11, 12)
+        nc.sync.dma_start(offs_t[:], offs)
+        load_words(PARTNER, 0, QUAD)
+        load_scale_rows(nc.sync, ws[PARTNER], PLANE[PARTNER], wp_scales)
+        load_words(TOKEN, 0, 2)
+        load_scale_rows(nc.sync, ws[TOKEN], PLANE[TOKEN], w1_scales)
+        load_words(TOKEN, 2, QUAD)
+        for e0 in range(QUAD, E - 2, 2):
+            load_words(PARTNER, e0, e0 + 2)
+            load_words(TOKEN, e0, e0 + 2)
+        load_words(PARTNER, E - 2, E)
+        load_words(TOKEN, E - 2, E - 1)
+        load_words(TOKEN, E - 1, E)
         load_w2(0, 4)
         nc.sync.dma_start(pos1_t[:], pos1)
         load_w2(4, 8)
@@ -148,49 +115,79 @@ def tile_moe_duo_silu_kernel(
         lists = (offs_t, offs2_t)
         gw = {}
         gs = {}
-        for kind, a, e0, e1 in GATHERS:
+
+        def gather(a, e0, e1):
             offsets = lists[a][:, e0 * C // 16 : e1 * C // 16]
-            if kind == "w":
-                got = keep.tile([P, (e1 - e0) * C], U32, name=f"gw{a}_{e0}", align_bytes=256)
-                nc.vector.tensor_copy(got[:], xw[:].bitcast(U32).indirect(offsets))
-            else:
-                got = keep.tile([P, (e1 - e0) * C], U8, name=f"gs{a}_{e0}", align_bytes=256)
-                nc.vector.tensor_copy(got[:], xs[:].indirect(offsets))
+            words = keep.tile([P, (e1 - e0) * C], U32, name=f"gw{a}_{e0}", align_bytes=256)
+            nc.vector.tensor_copy(words[:], xw[:].bitcast(U32).indirect(offsets))
+            scale_bytes = keep.tile([P, (e1 - e0) * C], U8, name=f"gs{a}_{e0}", align_bytes=256)
+            nc.vector.tensor_copy(scale_bytes[:], xs[:].indirect(offsets))
             for e in range(e0, e1):
-                (gw if kind == "w" else gs)[a, e] = got[:, (e - e0) * C : (e - e0 + 1) * C]
+                gw[a, e] = words[:, (e - e0) * C : (e - e0 + 1) * C]
+                gs[a, e] = scale_bytes[:, (e - e0) * C : (e - e0 + 1) * C]
+
+        gather(PARTNER, 0, QUAD)
+        gather(TOKEN, 0, 2)
+        gather(TOKEN, 2, QUAD)
+        for e0 in range(QUAD, E, 2):
+            gather(PARTNER, e0, e0 + 2)
+            gather(TOKEN, e0, e0 + 2)
 
         hq = keep.tile([P, S * 4], BF16, name="hq", align_bytes=256)
         hs = {}
-        for (first_e, last_e), turns in zip(TRIPLES, TURNS_AFTER):
-            for e in range(first_e, last_e):
-                acc = psum.tile([P, H], F32, name=f"acc{e}", offset=(e % 6) * BANK)
-                g, j = divmod(e, 4)
-                for a in range(2):
-                    nc.tensor.matmul_mx(
-                        out=acc[:],
-                        lhsT=gw[a, e].bitcast(FP8X4),
-                        lhsT_scale=gs[a, e],
-                        rhs=wa[a][:, e, :].bitcast(FP8X4),
-                        rhs_scale=ws[a][g][4 * j :, :],
-                        start=(a == 0),
-                        stop=(a == 1),
-                    )
-                h = keep.tile([P, H], BF16, name=f"h{e}", align_bytes=256)
-                nc.scalar.activation(
-                    h[:].rearrange("s (u p d) -> s u p d", u=2, d=2), acc[:].rearrange("s (p u d) -> s u p d", u=2, d=2), SILU
-                )
-                hs[e] = h
-            for e0, e1, bank_no in turns:
-                count = e1 - e0
-                turned = psum.tile([P, count, 2, C], F32, name=f"turned{e0}", offset=bank_no * BANK)
-                for e in range(e0, e1):
-                    for u in range(2):
-                        nc.tensor.transpose(turned[:, e - e0, u, :], hs[e][:].bitcast(F32)[:, u * P : (u + 1) * P], ident[:])
-                move = nc.vector.tensor_copy if e0 in VECTOR_TURNS else nc.scalar.copy
-                move(
-                    hq[:].bitcast(F32)[:, e0 * 2 * C : e1 * 2 * C].rearrange("p (x s u) -> p x s u", x=count, u=2),
-                    turned[:].rearrange("p x u s -> p x s u"),
-                )
+
+        def first_pass(target, a, e, cols):
+            nc.tensor.matmul_mx(
+                out=target,
+                lhsT=gw[a, e].bitcast(FP8X4),
+                lhsT_scale=gs[a, e],
+                rhs=wa[a][:, e, cols].bitcast(FP8X4),
+                rhs_scale=ws[a][PLANE[a] :, e, cols],
+                start=(a == PARTNER),
+                stop=(a == TOKEN),
+            )
+
+        def silu(e, source, p0, p1):
+            nc.scalar.activation(
+                hs[e][:].rearrange("s (u p d) -> s u p d", u=2, d=2)[:, :, p0:p1, :],
+                source.rearrange("s (p u d) -> s u p d", u=2, d=2),
+                SILU,
+            )
+
+        def turn(e, target):
+            for u in range(2):
+                nc.tensor.transpose(target[:, u * C : (u + 1) * C], hs[e][:].bitcast(F32)[:, u * P : (u + 1) * P], ident[:])
+
+        def weave(e, source):
+            move = nc.vector.tensor_copy if e in VECTOR_TURNS else nc.scalar.copy
+            move(
+                hq[:].bitcast(F32)[:, e * 2 * C : (e + 1) * 2 * C].rearrange("p (s u) -> p s u", u=2),
+                source.rearrange("p (u s) -> p s u", u=2),
+            )
+
+        halves = (slice(0, HALF), slice(HALF, H))
+        for e in range(0, E, 2):
+            base = 3 * (e // 2 % 2)
+            whole, low, high = [psum.tile([P, H], F32, name=f"bank{e}_{j}", offset=(base + j) * BANK) for j in range(3)]
+            for a in (PARTNER, TOKEN):
+                first_pass(whole[:], a, e, slice(0, H))
+                first_pass(low[:, :HALF], a, e + 1, halves[0])
+                first_pass(high[:, :HALF], a, e + 1, halves[1])
+            if e > 0:
+                turn(e - 2, low[:, HALF:])
+                turn(e - 1, high[:, HALF:])
+            for j in range(2):
+                hs[e + j] = keep.tile([P, H], BF16, name=f"h{e + j}", align_bytes=256)
+            silu(e, whole[:], 0, P)
+            silu(e + 1, low[:, :HALF], 0, P // 2)
+            silu(e + 1, high[:, :HALF], P // 2, P)
+            if e > 0:
+                weave(e - 2, low[:, HALF:])
+                weave(e - 1, high[:, HALF:])
+        for j in range(2):
+            spare = psum.tile([P, HALF], F32, name=f"spare{j}", offset=(6 + j) * BANK)
+            turn(E - 2 + j, spare[:])
+            weave(E - 2 + j, spare[:])
 
         y = keep.tile([P, S], F32, name="y")
         hc = {}
@@ -202,19 +199,19 @@ def tile_moe_duo_silu_kernel(
             for e in range(e0, e1):
                 mine = slice((e - e0) * C, (e - e0 + 1) * C)
                 hc[e] = (codes[:, mine], scales[:, mine])
-        for (e0, e1), bank_no in zip(Y_RUNS, Y_BANKS):
+        for bank_no, (e0, e1) in zip(Y_BANKS, Y_RUNS):
             bank = psum.tile([P, (e1 - e0) * C], F32, name=f"ybank{e0}", offset=bank_no * BANK)
             for e in range(e0, e1):
                 nc.tensor.matmul_mx(
                     out=bank[:, (e - e0) * C : (e - e0 + 1) * C],
                     lhsT=w2[:, e, :].bitcast(FP8X4),
-                    lhsT_scale=w2s[:, e, :],
+                    lhsT_scale=w2s[W2_PLANE:, e, :],
                     rhs=hc[e][0].bitcast(FP8X4),
                     rhs_scale=hc[e][1],
                     start=True,
                     stop=True,
                 )
-            move = nc.vector.tensor_copy if e0 in VECTOR_Y else nc.scalar.copy
+            move = nc.scalar.copy if e0 in SCALAR_Y else nc.vector.tensor_copy
             move(y[:, e0 * C : e1 * C], bank[:])
 
         first = keep.tile([P, T], F32, name="first")

@@ -21,15 +21,12 @@ SILU = mybir.ActivationFunctionType.Silu
 
 TOKEN, PARTNER = 0, 1
 BANK = 2048
-PLANE = {TOKEN: 0, PARTNER: 4}
-W2_PLANE = 8
 QUANT_RUNS = ((0, 4), (4, 8), (8, 10), (10, 11), (11, 12))
 Y_RUNS = ((0, 4), (4, 8), (8, 11), (11, 12))
 SCALAR_Y = (4, 8)
 Y_BANKS = (0, 1, 2, 3)
 HALF = H // 2
 QUAD = 4
-VECTOR_TURNS = (8, 9)
 OUT_RUNS = ((0, 384), (384, 640), (640, 768))
 
 
@@ -48,29 +45,38 @@ def tile_moe_duo_silu_kernel(
         xw = keep.tile([P, T], I32, name="xw", align_bytes=64)
         xs = keep.tile([P, T], U8, name="xs", align_bytes=64)
         wa = [keep.tile([P, E, H], I32, name=f"wa{a}", align_bytes=256) for a in range(2)]
-        ws = [keep.tile([P, E, H], U8, name=f"ws{a}", align_bytes=256) for a in range(2)]
+        ws = [[keep.tile([P, H], U8, name=f"ws{a}_{g}", align_bytes=256) for g in range(E // QUAD)] for a in range(2)]
         w2 = keep.tile([P, E, N], I32, name="w2", align_bytes=256)
         w2s = keep.tile([P, E, N], U8, name="w2s", align_bytes=256)
         gates = [keep.tile([P, T], F32, name=f"gate{r}") for r in range(2)]
         ident = keep.tile([P, P], F32, name="ident", align_bytes=64)
 
         words_in = (w1_words, wp_words)
+        scales_in = (w1_scales, wp_scales)
 
         nc.gpsimd.memset(xs[:].bitcast(I32), 0)
-        nc.vector.memset(ws[PARTNER][:].rearrange("p e n -> p (e n)").bitcast(I32), 0)
-        nc.gpsimd.memset(ws[TOKEN][:].rearrange("p e n -> p (e n)").bitcast(I32), 0)
-        nc.gpsimd.memset(w2s[:].rearrange("p e n -> p (e n)").bitcast(I32), 0)
+        for g in range(E // QUAD):
+            for a in (PARTNER, TOKEN):
+                nc.vector.memset(ws[a][g][:].bitcast(I32), 0)
+        nc.vector.memset(w2s[:].rearrange("p e n -> p (e n)").bitcast(I32), 0)
 
         def load_words(a, e0, e1):
             nc.sync.dma_start(
                 out=wa[a][:, e0:e1, :], in_=words_in[a][e0:e1, 0].rearrange("e p n t -> p e (n t)").bitcast(I32)
             )
 
-        def load_scale_rows(queue, plane, first, source):
-            for r in range(4):
+        def load_scales(queue, a, g):
+            for q in range(4):
                 queue.dma_start(
-                    out=plane[first + r : P : 32, :, :].bitcast(I32),
-                    in_=source[:, 0].rearrange("e (q r) n -> r q e n", r=4)[r].bitcast(I32),
+                    out=ws[a][g][32 * q : 32 * q + 16, :].bitcast(I32),
+                    in_=scales_in[a][QUAD * g : QUAD * (g + 1), 0, 4 * q : 4 * q + 4, :].bitcast(I32),
+                )
+
+        def load_w2_scales():
+            for r in range(4):
+                nc.gpsimd.dma_start(
+                    out=w2s[r:P:32, :, :].bitcast(I32),
+                    in_=w2_scales[:, 0].rearrange("e (q r) n -> r q e n", r=4)[r].bitcast(I32),
                 )
 
         def load_xs(r):
@@ -87,23 +93,28 @@ def tile_moe_duo_silu_kernel(
         load_xs(2)
         load_xs(3)
         make_identity(nc, ident[:])
-        load_scale_rows(nc.gpsimd, w2s, W2_PLANE, w2_scales)
+        load_scales(nc.gpsimd, PARTNER, 1)
+        load_scales(nc.gpsimd, PARTNER, 2)
+        load_scales(nc.gpsimd, TOKEN, 2)
+        load_w2_scales()
         nc.sync.dma_start(out=xw[:], in_=x_words[0].rearrange("p t d -> p (t d)").bitcast(I32))
         load_xs(0)
         load_xs(1)
         nc.sync.dma_start(offs2_t[:], offs2)
         nc.sync.dma_start(offs_t[:], offs)
         load_words(PARTNER, 0, QUAD)
-        load_scale_rows(nc.sync, ws[PARTNER], PLANE[PARTNER], wp_scales)
-        load_words(TOKEN, 0, 2)
-        load_scale_rows(nc.sync, ws[TOKEN], PLANE[TOKEN], w1_scales)
-        load_words(TOKEN, 2, QUAD)
-        for e0 in range(QUAD, E - 2, 2):
-            load_words(PARTNER, e0, e0 + 2)
-            load_words(TOKEN, e0, e0 + 2)
-        load_words(PARTNER, E - 2, E)
-        load_words(TOKEN, E - 2, E - 1)
-        load_words(TOKEN, E - 1, E)
+        load_scales(nc.sync, PARTNER, 0)
+        load_words(TOKEN, 0, QUAD)
+        load_scales(nc.sync, TOKEN, 0)
+        load_words(PARTNER, QUAD, 2 * QUAD)
+        load_scales(nc.sync, TOKEN, 1)
+        load_words(TOKEN, 4, 6)
+        load_words(TOKEN, 6, 8)
+        load_words(PARTNER, 8, 10)
+        load_words(TOKEN, 8, 10)
+        for e in range(E - 2, E):
+            load_words(PARTNER, e, e + 1)
+            load_words(TOKEN, e, e + 1)
         load_w2(0, 4)
         nc.sync.dma_start(pos1_t[:], pos1)
         load_w2(4, 8)
@@ -129,9 +140,12 @@ def tile_moe_duo_silu_kernel(
         gather(PARTNER, 0, QUAD)
         gather(TOKEN, 0, 2)
         gather(TOKEN, 2, QUAD)
-        for e0 in range(QUAD, E, 2):
+        for e0 in range(QUAD, E - 2, 2):
             gather(PARTNER, e0, e0 + 2)
             gather(TOKEN, e0, e0 + 2)
+        for e in range(E - 2, E):
+            gather(PARTNER, e, e + 1)
+            gather(TOKEN, e, e + 1)
 
         hq = keep.tile([P, S * 4], BF16, name="hq", align_bytes=256)
         hs = {}
@@ -142,7 +156,7 @@ def tile_moe_duo_silu_kernel(
                 lhsT=gw[a, e].bitcast(FP8X4),
                 lhsT_scale=gs[a, e],
                 rhs=wa[a][:, e, cols].bitcast(FP8X4),
-                rhs_scale=ws[a][PLANE[a] :, e, cols],
+                rhs_scale=ws[a][e // QUAD][4 * (e % QUAD) :, cols],
                 start=(a == PARTNER),
                 stop=(a == TOKEN),
             )
@@ -159,8 +173,7 @@ def tile_moe_duo_silu_kernel(
                 nc.tensor.transpose(target[:, u * C : (u + 1) * C], hs[e][:].bitcast(F32)[:, u * P : (u + 1) * P], ident[:])
 
         def weave(e, source):
-            move = nc.vector.tensor_copy if e in VECTOR_TURNS else nc.scalar.copy
-            move(
+            nc.scalar.copy(
                 hq[:].bitcast(F32)[:, e * 2 * C : (e + 1) * 2 * C].rearrange("p (s u) -> p s u", u=2),
                 source.rearrange("p (u s) -> p s u", u=2),
             )
@@ -169,18 +182,27 @@ def tile_moe_duo_silu_kernel(
         for e in range(0, E, 2):
             base = 3 * (e // 2 % 2)
             whole, low, high = [psum.tile([P, H], F32, name=f"bank{e}_{j}", offset=(base + j) * BANK) for j in range(3)]
-            for a in (PARTNER, TOKEN):
-                first_pass(whole[:], a, e, slice(0, H))
-                first_pass(low[:, :HALF], a, e + 1, halves[0])
-                first_pass(high[:, :HALF], a, e + 1, halves[1])
-            if e > 0:
-                turn(e - 2, low[:, HALF:])
-                turn(e - 1, high[:, HALF:])
+            in_one = e if e < E - 2 else e + 1
             for j in range(2):
                 hs[e + j] = keep.tile([P, H], BF16, name=f"h{e + j}", align_bytes=256)
-            silu(e, whole[:], 0, P)
-            silu(e + 1, low[:, :HALF], 0, P // 2)
-            silu(e + 1, high[:, :HALF], P // 2, P)
+            order = [(a, x) for a in (PARTNER, TOKEN) for x in (e, e + 1)]
+            if e == E - 2:
+                order = [(a, x) for x in (e, e + 1) for a in (PARTNER, TOKEN)]
+            for a, x in order:
+                if x == in_one:
+                    first_pass(whole[:], a, x, slice(0, H))
+                else:
+                    first_pass(low[:, :HALF], a, x, halves[0])
+                    first_pass(high[:, :HALF], a, x, halves[1])
+                    if a == TOKEN and e > 0:
+                        turn(e - 2, low[:, HALF:])
+                        turn(e - 1, high[:, HALF:])
+            for x in (e, e + 1):
+                if x == in_one:
+                    silu(x, whole[:], 0, P)
+                else:
+                    silu(x, low[:, :HALF], 0, P // 2)
+                    silu(x, high[:, :HALF], P // 2, P)
             if e > 0:
                 weave(e - 2, low[:, HALF:])
                 weave(e - 1, high[:, HALF:])
@@ -205,7 +227,7 @@ def tile_moe_duo_silu_kernel(
                 nc.tensor.matmul_mx(
                     out=bank[:, (e - e0) * C : (e - e0 + 1) * C],
                     lhsT=w2[:, e, :].bitcast(FP8X4),
-                    lhsT_scale=w2s[W2_PLANE:, e, :],
+                    lhsT_scale=w2s[:, e, :],
                     rhs=hc[e][0].bitcast(FP8X4),
                     rhs_scale=hc[e][1],
                     start=True,

@@ -18,6 +18,7 @@ FP8X4 = mybir.dt.float8_e4m3fn_x4
 MULT = mybir.AluOpType.mult
 ADD = mybir.AluOpType.add
 SILU = mybir.ActivationFunctionType.Silu
+COPY = mybir.ActivationFunctionType.Copy
 
 TOKEN, PARTNER = 0, 1
 BANK = 2048
@@ -27,7 +28,7 @@ SCALAR_Y = (4, 8)
 Y_BANKS = (0, 1, 2, 3)
 HALF = H // 2
 QUAD = 4
-OUT_RUNS = ((0, 384), (384, 640), (640, 768))
+FUSED = 512
 
 
 def tile_moe_duo_silu_kernel(
@@ -48,7 +49,7 @@ def tile_moe_duo_silu_kernel(
         ws = [[keep.tile([P, H], U8, name=f"ws{a}_{g}", align_bytes=256) for g in range(E // QUAD)] for a in range(2)]
         w2 = keep.tile([P, E, N], I32, name="w2", align_bytes=256)
         w2s = keep.tile([P, E, N], U8, name="w2s", align_bytes=256)
-        gates = [keep.tile([P, T], F32, name=f"gate{r}") for r in range(2)]
+        gates = keep.tile([P, 2, T], F32, name="gates")
         ident = keep.tile([P, P], F32, name="ident", align_bytes=64)
 
         words_in = (w1_words, wp_words)
@@ -120,8 +121,8 @@ def tile_moe_duo_silu_kernel(
         load_w2(4, 8)
         nc.sync.dma_start(pos2_t[:], pos2)
         load_w2(8, 12)
-        nc.sync.dma_start(out=gates[0][:], in_=gate[0])
-        nc.sync.dma_start(out=gates[1][:], in_=gate[1])
+        nc.sync.dma_start(out=gates[:, 0, :], in_=gate[0])
+        nc.sync.dma_start(out=gates[:, 1, :], in_=gate[1])
 
         lists = (offs_t, offs2_t)
         gw = {}
@@ -236,22 +237,28 @@ def tile_moe_duo_silu_kernel(
             move = nc.scalar.copy if e0 in SCALAR_Y else nc.vector.tensor_copy
             move(y[:, e0 * C : e1 * C], bank[:])
 
-        first = keep.tile([P, T], F32, name="first")
-        nc.vector.tensor_tensor(first[:], y[:].indirect(pos1_t[:]), gates[0][:], MULT)
-        seconds = {}
+        def fetch(pos_t, t0, t1, name):
+            raw = keep.tile([P, t1 - t0], F32, name=name)
+            nc.scalar.activation(raw[:], y[:].indirect(pos_t[:, t0 // 16 : t1 // 16]), COPY)
+            return raw
 
-        def gather_second(t0, t1):
-            second = keep.tile([P, t1 - t0], F32, name=f"second{t0}")
-            nc.vector.tensor_tensor(second[:], y[:].indirect(pos2_t[:, t0 // 16 : t1 // 16]), gates[1][:, t0:t1], MULT)
-            seconds[t0] = second
+        def weigh(term, raw, r, t0, t1):
+            nc.vector.tensor_tensor(term[:, t0:t1], raw[:], gates[:, r, t0:t1], MULT)
 
         def add_and_store(t0, t1):
-            total = keep.tile([P, t1 - t0], F32, name=f"total{t0}")
-            nc.vector.tensor_tensor(total[:], first[:, t0:t1], seconds[t0][:], ADD)
-            nc.sync.dma_start(out=out[:, t0:t1], in_=total[:])
+            nc.vector.tensor_tensor(total[:, t0:t1], first[:, t0:t1], second[:, t0:t1], ADD)
+            nc.sync.dma_start(out=out[:, t0:t1], in_=total[:, t0:t1])
 
-        gather_second(*OUT_RUNS[0])
-        for done, ahead in zip(OUT_RUNS, OUT_RUNS[1:]):
-            gather_second(*ahead)
-            add_and_store(*done)
-        add_and_store(*OUT_RUNS[-1])
+        first = keep.tile([P, T], F32, name="first")
+        second = keep.tile([P, T], F32, name="second")
+        total = keep.tile([P, T], F32, name="total")
+        nc.vector.tensor_tensor(first[:, :FUSED], y[:].indirect(pos1_t[:, : FUSED // 16]), gates[:, 0, :FUSED], MULT)
+        raw_a = fetch(pos2_t, 0, FUSED, "raw_a")
+        raw_b = fetch(pos2_t, FUSED, T, "raw_b")
+        raw_c = fetch(pos1_t, FUSED, T, "raw_c")
+        weigh(second, raw_a, 1, 0, FUSED)
+        weigh(second, raw_b, 1, FUSED, T)
+        add_and_store(0, FUSED // 2)
+        weigh(first, raw_c, 0, FUSED, T)
+        add_and_store(FUSED // 2, FUSED)
+        add_and_store(FUSED, T)

@@ -81,7 +81,7 @@ def tile_moe_duo_silu_kernel(
                 )
 
         def load_xs(r):
-            queue = nc.sync if r < 2 else nc.scalar
+            queue = nc.sync if r < 1 else nc.scalar
             queue.dma_start(
                 out=xs[r:P:32, :].bitcast(I32), in_=x_scales[0].rearrange("(q r) t -> r q t", r=4)[r].bitcast(I32)
             )
@@ -91,6 +91,7 @@ def tile_moe_duo_silu_kernel(
                 out=w2[:, e0:e1, :], in_=w2_words[e0:e1, 0].rearrange("e p n t -> p e (n t)").bitcast(I32)
             )
 
+        load_xs(1)
         load_xs(2)
         load_xs(3)
         make_identity(nc, ident[:])
@@ -100,19 +101,21 @@ def tile_moe_duo_silu_kernel(
         load_w2_scales()
         nc.sync.dma_start(out=xw[:], in_=x_words[0].rearrange("p t d -> p (t d)").bitcast(I32))
         load_xs(0)
-        load_xs(1)
         nc.sync.dma_start(offs2_t[:], offs2)
         nc.sync.dma_start(offs_t[:], offs)
         load_words(PARTNER, 0, QUAD)
         load_scales(nc.sync, PARTNER, 0)
-        load_words(TOKEN, 0, QUAD)
+        load_words(TOKEN, 0, 2)
         load_scales(nc.sync, TOKEN, 0)
-        load_words(PARTNER, QUAD, 2 * QUAD)
+        load_words(TOKEN, 2, 4)
+        load_words(PARTNER, 4, 6)
         load_scales(nc.sync, TOKEN, 1)
         load_words(TOKEN, 4, 6)
+        load_words(PARTNER, 6, 8)
         load_words(TOKEN, 6, 8)
         load_words(PARTNER, 8, 10)
-        load_words(TOKEN, 8, 10)
+        load_words(TOKEN, 8, 9)
+        load_words(TOKEN, 9, 10)
         for e in range(E - 2, E):
             load_words(PARTNER, e, e + 1)
             load_words(TOKEN, e, e + 1)
@@ -141,9 +144,12 @@ def tile_moe_duo_silu_kernel(
         gather(PARTNER, 0, QUAD)
         gather(TOKEN, 0, 2)
         gather(TOKEN, 2, QUAD)
-        for e0 in range(QUAD, E - 2, 2):
+        for e0 in range(QUAD, E - 4, 2):
             gather(PARTNER, e0, e0 + 2)
             gather(TOKEN, e0, e0 + 2)
+        gather(PARTNER, E - 4, E - 2)
+        gather(TOKEN, E - 4, E - 3)
+        gather(TOKEN, E - 3, E - 2)
         for e in range(E - 2, E):
             gather(PARTNER, e, e + 1)
             gather(TOKEN, e, e + 1)

@@ -112,7 +112,8 @@ def tile_moe_duo_silu_kernel(
         load_scales(nc.sync, TOKEN, 1)
         load_words(TOKEN, 4, 6)
         load_words(PARTNER, 6, 8)
-        load_words(TOKEN, 6, 8)
+        load_words(TOKEN, 6, 7)
+        load_words(TOKEN, 7, 8)
         load_words(PARTNER, 8, 10)
         load_words(TOKEN, 8, 9)
         load_words(TOKEN, 9, 10)
@@ -144,12 +145,12 @@ def tile_moe_duo_silu_kernel(
         gather(PARTNER, 0, QUAD)
         gather(TOKEN, 0, 2)
         gather(TOKEN, 2, QUAD)
-        for e0 in range(QUAD, E - 4, 2):
+        gather(PARTNER, 4, 6)
+        gather(TOKEN, 4, 6)
+        for e0 in (6, 8):
             gather(PARTNER, e0, e0 + 2)
-            gather(TOKEN, e0, e0 + 2)
-        gather(PARTNER, E - 4, E - 2)
-        gather(TOKEN, E - 4, E - 3)
-        gather(TOKEN, E - 3, E - 2)
+            gather(TOKEN, e0, e0 + 1)
+            gather(TOKEN, e0 + 1, e0 + 2)
         for e in range(E - 2, E):
             gather(PARTNER, e, e + 1)
             gather(TOKEN, e, e + 1)
@@ -188,10 +189,18 @@ def tile_moe_duo_silu_kernel(
         halves = (slice(0, HALF), slice(HALF, H))
         for e in range(0, E, 2):
             base = 3 * (e // 2 % 2)
-            whole, low, high = [psum.tile([P, H], F32, name=f"bank{e}_{j}", offset=(base + j) * BANK) for j in range(3)]
-            in_one = e if e < E - 2 else e + 1
             for j in range(2):
                 hs[e + j] = keep.tile([P, H], BF16, name=f"h{e + j}", align_bytes=256)
+            if e == 8:
+                banks = [psum.tile([P, H], F32, name=f"bank{e}_{j}", offset=(base + j) * BANK) for j in range(2)]
+                for a in (PARTNER, TOKEN):
+                    for j in range(2):
+                        first_pass(banks[j][:], a, e + j, slice(0, H))
+                for j in range(2):
+                    silu(e + j, banks[j][:], 0, P)
+                continue
+            whole, low, high = [psum.tile([P, H], F32, name=f"bank{e}_{j}", offset=(base + j) * BANK) for j in range(3)]
+            in_one = e if e < E - 2 else e + 1
             order = [(a, x) for a in (PARTNER, TOKEN) for x in (e, e + 1)]
             if e == E - 2:
                 order = [(a, x) for x in (e, e + 1) for a in (PARTNER, TOKEN)]
@@ -213,10 +222,11 @@ def tile_moe_duo_silu_kernel(
             if e > 0:
                 weave(e - 2, low[:, HALF:])
                 weave(e - 1, high[:, HALF:])
-        for j in range(2):
-            spare = psum.tile([P, HALF], F32, name=f"spare{j}", offset=(6 + j) * BANK)
-            turn(E - 2 + j, spare[:])
-            weave(E - 2 + j, spare[:])
+            if e == 6 or e == E - 2:
+                for j in range(2):
+                    spare = psum.tile([P, HALF], F32, name=f"spare{e}_{j}", offset=(6 + j) * BANK)
+                    turn(e + j, spare[:])
+                    weave(e + j, spare[:])
 
         y = keep.tile([P, S], F32, name="y")
         hc = {}

@@ -28,6 +28,7 @@ SCALAR_Y = (4, 8)
 Y_BANKS = (0, 1, 2, 3)
 HALF = H // 2
 QUAD = 4
+W2_ROW = 4
 FUSED = 512
 
 
@@ -76,7 +77,7 @@ def tile_moe_duo_silu_kernel(
         def load_w2_scales():
             for r in range(4):
                 nc.gpsimd.dma_start(
-                    out=w2s[r:P:32, :, :].bitcast(I32),
+                    out=w2s[W2_ROW + r : P : 32, :, :].bitcast(I32),
                     in_=w2_scales[:, 0].rearrange("e (q r) n -> r q e n", r=4)[r].bitcast(I32),
                 )
 
@@ -109,8 +110,8 @@ def tile_moe_duo_silu_kernel(
         load_scales(nc.sync, TOKEN, 0)
         load_words(TOKEN, 2, 4)
         load_words(PARTNER, 4, 6)
-        load_scales(nc.sync, TOKEN, 1)
         load_words(TOKEN, 4, 6)
+        load_scales(nc.sync, TOKEN, 1)
         load_words(PARTNER, 6, 8)
         load_words(TOKEN, 6, 7)
         load_words(TOKEN, 7, 8)
@@ -244,7 +245,7 @@ def tile_moe_duo_silu_kernel(
                 nc.tensor.matmul_mx(
                     out=bank[:, (e - e0) * C : (e - e0 + 1) * C],
                     lhsT=w2[:, e, :].bitcast(FP8X4),
-                    lhsT_scale=w2s[:, e, :],
+                    lhsT_scale=w2s[W2_ROW:, e, :],
                     rhs=hc[e][0].bitcast(FP8X4),
                     rhs_scale=hc[e][1],
                     start=True,

@@ -76,7 +76,7 @@ def tile_moe_duo_silu_kernel(
 
         def load_w2_scales():
             for r in range(4):
-                nc.gpsimd.dma_start(
+                nc.sync.dma_start(
                     out=w2s[W2_ROW + r : P : 32, :, :].bitcast(I32),
                     in_=w2_scales[:, 0].rearrange("e (q r) n -> r q e n", r=4)[r].bitcast(I32),
                 )
@@ -99,7 +99,6 @@ def tile_moe_duo_silu_kernel(
         load_scales(nc.gpsimd, PARTNER, 1)
         load_scales(nc.gpsimd, PARTNER, 2)
         load_scales(nc.gpsimd, TOKEN, 2)
-        load_w2_scales()
         nc.sync.dma_start(out=xw[:], in_=x_words[0].rearrange("p t d -> p (t d)").bitcast(I32))
         load_xs(0)
         nc.sync.dma_start(offs2_t[:], offs2)
@@ -121,6 +120,7 @@ def tile_moe_duo_silu_kernel(
         for e in range(E - 2, E):
             load_words(PARTNER, e, e + 1)
             load_words(TOKEN, e, e + 1)
+        load_w2_scales()
         load_w2(0, 4)
         nc.sync.dma_start(pos1_t[:], pos1)
         load_w2(4, 8)

from contextlib import ExitStack

import concourse.mybir as mybir
from concourse.masks import make_identity

K, T, E, C, H, N = 512, 768, 12, 128, 512, 128
S = E * C
P = 128
FLOPS = 2 * S * (2 * K * H + H * N)

F32 = mybir.dt.float32
BF16 = mybir.dt.bfloat16
I32 = mybir.dt.int32
U32 = mybir.dt.uint32
U16 = mybir.dt.uint16
U8 = mybir.dt.uint8
FP8X4 = mybir.dt.float8_e4m3fn_x4
MULT = mybir.AluOpType.mult
ADD = mybir.AluOpType.add
SILU = mybir.ActivationFunctionType.Silu
COPY = mybir.ActivationFunctionType.Copy

TOKEN, PARTNER = 0, 1
BANK = 2048
QUANT_RUNS = ((0, 4), (4, 8), (8, 10), (10, 11), (11, 12))
Y_RUNS = ((0, 4), (4, 8), (8, 11), (11, 12))
SCALAR_Y = (4, 8)
Y_BANKS = (0, 1, 2, 3)
HALF = H // 2
QUAD = 4
W2_ROW = 4
FUSED = 512


def tile_moe_duo_silu_kernel(
    tc, x_words, x_scales, w1_words, w1_scales, wp_words, wp_scales, w2_words, w2_scales, gate, offs, pos1, pos2, offs2, out
):
    nc = tc.nc
    with ExitStack() as ctx:
        keep = ctx.enter_context(tc.tile_pool(name="keep", bufs=1))
        psum = ctx.enter_context(tc.psum_pool(name="psum", bufs=1))

        offs_t = keep.tile([P, S // 16], U16, name="offs_t")
        offs2_t = keep.tile([P, S // 16], U16, name="offs2_t")
        pos1_t = keep.tile([P, T // 16], U16, name="pos1_t")
        pos2_t = keep.tile([P, T // 16], U16, name="pos2_t")
        xw = keep.tile([P, T], I32, name="xw", align_bytes=64)
        xs = keep.tile([P, T], U8, name="xs", align_bytes=64)
        wa = [keep.tile([P, E, H], I32, name=f"wa{a}", align_bytes=256) for a in range(2)]
        ws = [[keep.tile([P, H], U8, name=f"ws{a}_{g}", align_bytes=256) for g in range(E // QUAD)] for a in range(2)]
        w2 = keep.tile([P, E, N], I32, name="w2", align_bytes=256)
        w2s = keep.tile([P, E, N], U8, name="w2s", align_bytes=256)
        gates = keep.tile([P, 2, T], F32, name="gates")
        ident = keep.tile([P, P], F32, name="ident", align_bytes=64)

        words_in = (w1_words, wp_words)
        scales_in = (w1_scales, wp_scales)

        nc.gpsimd.memset(xs[:].bitcast(I32), 0)
        for g in range(E // QUAD):
            for a in (PARTNER, TOKEN):
                nc.vector.memset(ws[a][g][:].bitcast(I32), 0)
        nc.vector.memset(w2s[:].rearrange("p e n -> p (e n)").bitcast(I32), 0)

        def load_words(a, e0, e1):
            nc.sync.dma_start(
                out=wa[a][:, e0:e1, :], in_=words_in[a][e0:e1, 0].rearrange("e p n t -> p e (n t)").bitcast(I32)
            )

        def load_scales(queue, a, g):
            for q in range(4):
                queue.dma_start(
                    out=ws[a][g][32 * q : 32 * q + 16, :].bitcast(I32),
                    in_=scales_in[a][QUAD * g : QUAD * (g + 1), 0, 4 * q : 4 * q + 4, :].bitcast(I32),
                )

        def load_w2_scales():
            for r in range(4):
                nc.sync.dma_start(
                    out=w2s[W2_ROW + r : P : 32, :, :].bitcast(I32),
                    in_=w2_scales[:, 0].rearrange("e (q r) n -> r q e n", r=4)[r].bitcast(I32),
                )

        def load_xs(r):
            queue = nc.sync if r < 1 else nc.scalar
            queue.dma_start(
                out=xs[r:P:32, :].bitcast(I32), in_=x_scales[0].rearrange("(q r) t -> r q t", r=4)[r].bitcast(I32)
            )

        def load_w2(e0, e1):
            nc.sync.dma_start(
                out=w2[:, e0:e1, :], in_=w2_words[e0:e1, 0].rearrange("e p n t -> p e (n t)").bitcast(I32)
            )

        load_xs(1)
        load_xs(2)
        load_xs(3)
        make_identity(nc, ident[:])
        load_scales(nc.gpsimd, PARTNER, 1)
        load_scales(nc.gpsimd, PARTNER, 2)
        load_scales(nc.gpsimd, TOKEN, 2)
        nc.sync.dma_start(out=xw[:], in_=x_words[0].rearrange("p t d -> p (t d)").bitcast(I32))
        load_xs(0)
        nc.sync.dma_start(offs2_t[:], offs2)
        nc.sync.dma_start(offs_t[:], offs)
        load_words(PARTNER, 0, QUAD)
        load_scales(nc.sync, PARTNER, 0)
        load_words(TOKEN, 0, 2)
        load_scales(nc.sync, TOKEN, 0)
        load_words(TOKEN, 2, 4)
        load_words(PARTNER, 4, 6)
        load_words(TOKEN, 4, 6)
        load_scales(nc.sync, TOKEN, 1)
        load_words(PARTNER, 6, 8)
        load_words(TOKEN, 6, 7)
        load_words(TOKEN, 7, 8)
        load_words(PARTNER, 8, 10)
        load_words(TOKEN, 8, 9)
        load_words(TOKEN, 9, 10)
        for e in range(E - 2, E):
            load_words(PARTNER, e, e + 1)
            load_words(TOKEN, e, e + 1)
        load_w2_scales()
        load_w2(0, 4)
        nc.sync.dma_start(pos1_t[:], pos1)
        load_w2(4, 8)
        nc.sync.dma_start(pos2_t[:], pos2)
        load_w2(8, 12)
        nc.sync.dma_start(out=gates[:, 0, :], in_=gate[0])
        nc.sync.dma_start(out=gates[:, 1, :], in_=gate[1])

        lists = (offs_t, offs2_t)
        gw = {}
        gs = {}

        def gather(a, e0, e1):
            offsets = lists[a][:, e0 * C // 16 : e1 * C // 16]
            words = keep.tile([P, (e1 - e0) * C], U32, name=f"gw{a}_{e0}", align_bytes=256)
            nc.vector.tensor_copy(words[:], xw[:].bitcast(U32).indirect(offsets))
            scale_bytes = keep.tile([P, (e1 - e0) * C], U8, name=f"gs{a}_{e0}", align_bytes=256)
            nc.vector.tensor_copy(scale_bytes[:], xs[:].indirect(offsets))
            for e in range(e0, e1):
                gw[a, e] = words[:, (e - e0) * C : (e - e0 + 1) * C]
                gs[a, e] = scale_bytes[:, (e - e0) * C : (e - e0 + 1) * C]

        gather(PARTNER, 0, QUAD)
        gather(TOKEN, 0, 2)
        gather(TOKEN, 2, QUAD)
        gather(PARTNER, 4, 6)
        gather(TOKEN, 4, 6)
        for e0 in (6, 8):
            gather(PARTNER, e0, e0 + 2)
            gather(TOKEN, e0, e0 + 1)
            gather(TOKEN, e0 + 1, e0 + 2)
        for e in range(E - 2, E):
            gather(PARTNER, e, e + 1)
            gather(TOKEN, e, e + 1)

        hq = keep.tile([P, S * 4], BF16, name="hq", align_bytes=256)
        hs = {}

        def first_pass(target, a, e, cols):
            nc.tensor.matmul_mx(
                out=target,
                lhsT=gw[a, e].bitcast(FP8X4),
                lhsT_scale=gs[a, e],
                rhs=wa[a][:, e, cols].bitcast(FP8X4),
                rhs_scale=ws[a][e // QUAD][4 * (e % QUAD) :, cols],
                start=(a == PARTNER),
                stop=(a == TOKEN),
            )

        def silu(e, source, p0, p1):
            nc.scalar.activation(
                hs[e][:].rearrange("s (u p d) -> s u p d", u=2, d=2)[:, :, p0:p1, :],
                source.rearrange("s (p u d) -> s u p d", u=2, d=2),
                SILU,
            )

        def turn(e, target):
            for u in range(2):
                nc.tensor.transpose(target[:, u * C : (u + 1) * C], hs[e][:].bitcast(F32)[:, u * P : (u + 1) * P], ident[:])

        def weave(e, source):
            nc.scalar.copy(
                hq[:].bitcast(F32)[:, e * 2 * C : (e + 1) * 2 * C].rearrange("p (s u) -> p s u", u=2),
                source.rearrange("p (u s) -> p s u", u=2),
            )

        halves = (slice(0, HALF), slice(HALF, H))
        for e in range(0, E, 2):
            base = 3 * (e // 2 % 2)
            for j in range(2):
                hs[e + j] = keep.tile([P, H], BF16, name=f"h{e + j}", align_bytes=256)
            if e == 8:
                banks = [psum.tile([P, H], F32, name=f"bank{e}_{j}", offset=(base + j) * BANK) for j in range(2)]
                for a in (PARTNER, TOKEN):
                    for j in range(2):
                        first_pass(banks[j][:], a, e + j, slice(0, H))
                for j in range(2):
                    silu(e + j, banks[j][:], 0, P)
                continue
            whole, low, high = [psum.tile([P, H], F32, name=f"bank{e}_{j}", offset=(base + j) * BANK) for j in range(3)]
            in_one = e if e < E - 2 else e + 1
            order = [(a, x) for a in (PARTNER, TOKEN) for x in (e, e + 1)]
            if e == E - 2:
                order = [(a, x) for x in (e, e + 1) for a in (PARTNER, TOKEN)]
            for a, x in order:
                if x == in_one:
                    first_pass(whole[:], a, x, slice(0, H))
                else:
                    first_pass(low[:, :HALF], a, x, halves[0])
                    first_pass(high[:, :HALF], a, x, halves[1])
                    if a == TOKEN and e > 0:
                        turn(e - 2, low[:, HALF:])
                        turn(e - 1, high[:, HALF:])
            for x in (e, e + 1):
                if x == in_one:
                    silu(x, whole[:], 0, P)
                else:
                    silu(x, low[:, :HALF], 0, P // 2)
                    silu(x, high[:, :HALF], P // 2, P)
            if e > 0:
                weave(e - 2, low[:, HALF:])
                weave(e - 1, high[:, HALF:])
            if e == 6 or e == E - 2:
                for j in range(2):
                    spare = psum.tile([P, HALF], F32, name=f"spare{e}_{j}", offset=(6 + j) * BANK)
                    turn(e + j, spare[:])
                    weave(e + j, spare[:])

        y = keep.tile([P, S], F32, name="y")
        hc = {}
        for e0, e1 in QUANT_RUNS:
            width = (e1 - e0) * C
            codes = keep.tile([P, width], U32, name=f"hc{e0}", align_bytes=256)
            scales = keep.tile([P, width], U8, name=f"hsc{e0}", align_bytes=256)
            nc.vector.quantize_mx(out=codes[:].bitcast(FP8X4), scales=scales[:], in_=hq[:, e0 * 4 * C : e1 * 4 * C])
            for e in range(e0, e1):
                mine = slice((e - e0) * C, (e - e0 + 1) * C)
                hc[e] = (codes[:, mine], scales[:, mine])
        for bank_no, (e0, e1) in zip(Y_BANKS, Y_RUNS):
            bank = psum.tile([P, (e1 - e0) * C], F32, name=f"ybank{e0}", offset=bank_no * BANK)
            for e in range(e0, e1):
                nc.tensor.matmul_mx(
                    out=bank[:, (e - e0) * C : (e - e0 + 1) * C],
                    lhsT=w2[:, e, :].bitcast(FP8X4),
                    lhsT_scale=w2s[W2_ROW:, e, :],
                    rhs=hc[e][0].bitcast(FP8X4),
                    rhs_scale=hc[e][1],
                    start=True,
                    stop=True,
                )
            move = nc.scalar.copy if e0 in SCALAR_Y else nc.vector.tensor_copy
            move(y[:, e0 * C : e1 * C], bank[:])

        def fetch(pos_t, t0, t1, name):
            raw = keep.tile([P, t1 - t0], F32, name=name)
            nc.scalar.activation(raw[:], y[:].indirect(pos_t[:, t0 // 16 : t1 // 16]), COPY)
            return raw

        def weigh(term, raw, r, t0, t1):
            nc.vector.tensor_tensor(term[:, t0:t1], raw[:], gates[:, r, t0:t1], MULT)

        def add_and_store(t0, t1):
            nc.vector.tensor_tensor(total[:, t0:t1], first[:, t0:t1], second[:, t0:t1], ADD)
            nc.sync.dma_start(out=out[:, t0:t1], in_=total[:, t0:t1])

        first = keep.tile([P, T], F32, name="first")
        second = keep.tile([P, T], F32, name="second")
        total = keep.tile([P, T], F32, name="total")
        nc.vector.tensor_tensor(first[:, :FUSED], y[:].indirect(pos1_t[:, : FUSED // 16]), gates[:, 0, :FUSED], MULT)
        raw_a = fetch(pos2_t, 0, FUSED, "raw_a")
        raw_b = fetch(pos2_t, FUSED, T, "raw_b")
        raw_c = fetch(pos1_t, FUSED, T, "raw_c")
        weigh(second, raw_a, 1, 0, FUSED)
        weigh(second, raw_b, 1, FUSED, T)
        add_and_store(0, FUSED // 2)
        weigh(first, raw_c, 0, FUSED, T)
        add_and_store(FUSED // 2, FUSED)
        add_and_store(FUSED, T)
